import numpy as np, ml_dtypes
CORES = [33,38,57,62,81,86,161,166,185,190,209,214]
N = 12
KT, FB, TK = 1, 32, 256
def setup_inputs(rng):
    return {"x": rng.standard_normal((N, 128, KT * TK), dtype=np.float32).astype(ml_dtypes.bfloat16), "w": rng.standard_normal((N, 128, KT * N * FB), dtype=np.float32).astype(ml_dtypes.bfloat16)}
def setup_inputs_big(rng):
    d = setup_inputs(rng)
    for k in ("x", "w"): d[k] = (d[k].astype(np.float32) * 1024.0).astype(d[k].dtype)
    return d
def setup_inputs_small(rng):
    d = setup_inputs(rng)
    for k in ("x", "w"): d[k] = (d[k].astype(np.float32) * (1 / 1024.0)).astype(d[k].dtype)
    return d
def reference(x, w):
    X, W = x.astype(np.float64), w.astype(np.float64)
    y = np.zeros((N, FB, N * TK))
    for j in range(N):
        for r in range(N):
            for t in range(KT):
                y[r][:, TK * j:TK * j + TK] += W[j][:, FB * (N * t + r):FB * (N * t + r) + FB].T @ X[j][:, TK * t:TK * t + TK]
    return {"y": y.astype(ml_dtypes.bfloat16 if x.dtype != np.float64 else np.float64)}

@@ -1,0 +1,150 @@
+from concourse.bass import DstId, RemoteDMATransfer
+
+N, FB, TK = 12, 32, 256
+PER_CHIP = 2
+NCHIP = N // PER_CHIP
+PHASES = NCHIP // 2
+SLOTS = 2 * PER_CHIP
+CW = PER_CHIP * FB
+ROWS, WID = 128, FB * TK // 128
+
+SCRATCH = {
+    "xs": ("sbuf", [128, TK], "bfloat16"),
+    "ws": ("sbuf", [128, N * FB], "bfloat16"),
+    "acc": ("psum", [128, 512 * PHASES], "float32"),
+    "prod": ("sbuf", [128, TK * PHASES], "bfloat16"),
+    "stage": ("dram", [N, ROWS, WID], "bfloat16"),
+    "land": ("dram", [N, ROWS, WID], "bfloat16"),
+}
+SEMAPHORES = (["ldx", "ldw", "sent", "fin0", "fin1"]
+              + ["%s%d" % (n, p) for n in ("mm", "cp", "st", "rel") for p in range(PHASES)]
+              + ["arr%d" % j for j in range(N)])
+
+
+def _pool(topo, src, dsts):
+    mask = topo.mask(src, dsts[0])
+    for d in dsts:
+        mask &= topo.mask(src, d)
+    return [e for e in range(mask.bit_length()) if (mask >> e) & 1]
+
+
+def _deal(pool, k):
+    per = 1
+    while per * 2 * k <= len(pool):
+        per *= 2
+    return [sum(1 << e for e in pool[i * per:(i + 1) * per]) for i in range(k)], per
+
+
+def _plan(cores, topo):
+    def place(c):
+        return (topo.host(c), topo.chip(c))
+    chips = [list(range(i, i + PER_CHIP)) for i in range(0, N, PER_CHIP)]
+    rep = [cores[m[0]] for m in chips]
+    world = range((max(topo.host(c) for c in cores) + 1) * topo.CORES_PER_HOST)
+    groups, calls, due = {}, {}, dict((r, {}) for r in range(N))
+    for j, s in enumerate(cores):
+        me = j // PER_CHIP
+        plane = [i for i in range(NCHIP) if i == me or topo.same_plane(rep[i], rep[me])]
+        far = [i for i in range(NCHIP) if i not in plane]
+        k = plane.index(me)
+        near = [plane[(k + t) % len(plane)] for t in range(1, len(plane))]
+        off = k * len(far) // len(plane)
+        far = [far[(off + t) % len(far)] for t in range(len(far))]
+        barred = [r for r in range(N) if r != j and not topo.may_write(s, cores[r])]
+        if barred:
+            seq = far + near
+        else:
+            at = [t * (NCHIP - 2) // len(far) for t in range(len(far))]
+            rest = list(near)
+            seq = [far[at.index(t)] if t in at else rest.pop(0) for t in range(NCHIP - 1)]
+        seq = seq + [me]
+        groups[j] = [tuple(sorted(seq[2 * p:2 * p + 2])) for p in range(PHASES)]
+        helpers = [h for h in world if place(h) == place(s) and h not in cores and topo.die(h) == topo.die(s)
+                   and all(topo.may_write(h, cores[r]) for r in barred)]
+        todo = []
+        for p, (a, b) in enumerate(groups[j]):
+            row = []
+            for pos, r in enumerate(chips[a] + chips[b]):
+                if r != j:
+                    via = helpers[(pos // PER_CHIP) % len(helpers)] if r in barred else None
+                    row.append((SLOTS * p + pos, r, via))
+            todo.append(row)
+        pool = _pool(topo, s, [cores[r] if via is None else via for row in todo for slot, r, via in row])
+        for p, row in enumerate(todo):
+            masks, per = _deal(pool, len(row))
+            trs, handed = [], {}
+            for (slot, r, via), m in zip(row, masks):
+                if via is None:
+                    trs.append((slot, cores[r], "land", j, "arr%d" % j, m, per))
+                    due[r][j] = (per, (0, p))
+                else:
+                    trs.append((slot, via, "stage", slot, "rel%d" % p, m, per))
+                    handed.setdefault(via, []).append((slot, r))
+            calls.setdefault(s, []).append(("st%d" % p, 16, trs))
+            for h, lst in handed.items():
+                hm, hper = _deal(_pool(topo, h, [cores[r] for slot, r in lst])[::2], len(lst))
+                calls.setdefault(h, []).append(("rel%d" % p, per * len(lst),
+                                                [(slot, cores[r], "land", j, "arr%d" % j, m, hper)
+                                                 for (slot, r), m in zip(lst, hm)]))
+                for slot, r in lst:
+                    due[r][j] = (hper, (1, p))
+    return groups, calls, due
+
+
+def rank_program(g, core, T, topo):
+    groups, calls, due = _plan(T.cores, topo)
+    S = T.sem
+    rank = T.rank_of(core)
+    queues = (g.sync, g.scalar)
+    stores = [0, 0]
+
+    if rank is not None:
+        g.sync.dma_start(out=T.xs[:], in_=T.x[:]).then_inc(S.ldx, 16)
+        g.scalar.dma_start(out=T.ws[:], in_=T.w[:]).then_inc(S.ldw, 16)
+        g.tensor.wait_ge(S.ldx, 16)
+        g.tensor.wait_ge(S.ldw, 16)
+        for p, (a, b) in enumerate(groups[rank]):
+            c0, c1 = 512 * p, 512 * p + TK
+            prod = T.prod[:, TK * p:TK * (p + 1)]
+            if b == a + 1:
+                parts = [(0, 2 * CW, a)]
+            else:
+                parts = [(0, CW, a), (CW, CW, b)]
+            for row, m, chip in parts:
+                g.tensor.matmul(T.acc[row:row + m, c0:c1], T.ws[:, CW * chip:CW * chip + m], T.xs[:],
+                                start=True, stop=True).then_inc(S["mm%d" % p], 1)
+            g.vector.wait_ge(S["mm%d" % p], len(parts))
+            g.vector.tensor_copy(out=prod, in_=T.acc[:, c0:c1]).then_inc(S["cp%d" % p], 1)
+            q = queues[p % 2]
+            q.wait_ge(S["cp%d" % p], 1)
+            q.dma_start(out=T.stage[SLOTS * p:SLOTS * (p + 1)], in_=prod).then_inc(S["st%d" % p], 16)
+        p = PHASES - 1
+        pos = PER_CHIP * groups[rank][p].index(rank // PER_CHIP) + rank % PER_CHIP
+        qi = (p + 1) % 2
+        queues[qi].wait_ge(S["cp%d" % p], 1)
+        queues[qi].dma_start(out=T.y[:, TK * rank:TK * (rank + 1)],
+                             in_=T.prod[FB * pos:FB * (pos + 1), TK * p:TK * (p + 1)]).then_inc(S["fin%d" % qi], 16)
+        stores[qi] += 1
+
+    total = 0
+    for sem, count, trs in calls.get(core, []):
+        g.wait_ge(S[sem], count)
+        lst = []
+        for slot, dst, buf, dslot, rsem, mask, per in trs:
+            rid, pid = topo.addr(dst, core)
+            lst.append(RemoteDMATransfer(dst_ids=[DstId(rid=rid, pnc=pid)], dma_engine_mask=mask, remote_sem=S[rsem],
+                                         src=T.stage[slot], dst=T[buf][dslot]))
+            total += per
+        g.remote_dma_fused(lst, local_sem=S.sent)
+
+    if rank is not None:
+        order = sorted(due[rank], key=lambda j: (due[rank][j][1], j))
+        for i, j in enumerate(order):
+            qi = i % 2
+            queues[qi].wait_ge(S["arr%d" % j], due[rank][j][0])
+            queues[qi].dma_start(out=T.y[:, TK * j:TK * (j + 1)], in_=T.land[j]).then_inc(S["fin%d" % qi], 16)
+            stores[qi] += 1
+        for qi in (0, 1):
+            queues[qi].wait_ge(S["fin%d" % qi], 16 * stores[qi])
+    if total:
+        g.wait_ge(S.sent, total)

@@ -14,6 +14,7 @@ SCRATCH = {
     "acc": ("psum", [128, 512 * PHASES], "float32"),
     "prod": ("sbuf", [128, TK * PHASES], "bfloat16"),
     "stage": ("dram", [N, ROWS, WID], "bfloat16"),
+    "hand": ("dram", [N - SLOTS, ROWS, WID], "bfloat16"),
     "land": ("dram", [N, ROWS, WID], "bfloat16"),
 }
 SEMAPHORES = (["ldx", "ldw", "sent", "fin0", "fin1"]
@@ -41,7 +42,7 @@ def _plan(cores, topo):
     chips = [list(range(i, i + PER_CHIP)) for i in range(0, N, PER_CHIP)]
     rep = [cores[m[0]] for m in chips]
     world = range((max(topo.host(c) for c in cores) + 1) * topo.CORES_PER_HOST)
-    groups, calls, due = {}, {}, dict((r, {}) for r in range(N))
+    groups, own, fwd, due = {}, {}, {}, dict((r, {}) for r in range(N))
     for j, s in enumerate(cores):
         me = j // PER_CHIP
         plane = [i for i in range(NCHIP) if i == me or topo.same_plane(rep[i], rep[me])]
@@ -59,15 +60,19 @@ def _plan(cores, topo):
             seq = [far[at.index(t)] if t in at else rest.pop(0) for t in range(NCHIP - 1)]
         seq = seq + [me]
         groups[j] = [tuple(sorted(seq[2 * p:2 * p + 2])) for p in range(PHASES)]
-        helpers = [h for h in world if place(h) == place(s) and h not in cores and topo.die(h) == topo.die(s)
-                   and all(topo.may_write(h, cores[r]) for r in barred)]
+        able = [h for h in world if place(h) == place(s) and h != s and all(topo.may_write(h, cores[r]) for r in barred)]
         todo = []
         for p, (a, b) in enumerate(groups[j]):
             row = []
             for pos, r in enumerate(chips[a] + chips[b]):
-                if r != j:
-                    via = helpers[(pos // PER_CHIP) % len(helpers)] if r in barred else None
-                    row.append((SLOTS * p + pos, r, via))
+                if r == j:
+                    continue
+                via = None
+                if r in barred:
+                    there = [h for h in able if topo.die(h) == topo.die(cores[r])]
+                    ranks = [h for h in there if h in cores]
+                    via = ranks[0] if ranks else there[p % len(there)]
+                row.append((SLOTS * p + pos, r, via))
             todo.append(row)
         pool = _pool(topo, s, [cores[r] if via is None else via for row in todo for slot, r, via in row])
         for p, row in enumerate(todo):
@@ -75,19 +80,21 @@ def _plan(cores, topo):
             trs, handed = [], {}
             for (slot, r, via), m in zip(row, masks):
                 if via is None:
-                    trs.append((slot, cores[r], "land", j, "arr%d" % j, m, per))
+                    trs.append(("stage", slot, cores[r], "land", j, "arr%d" % j, m, per))
                     due[r][j] = (per, (0, p))
                 else:
-                    trs.append((slot, via, "stage", slot, "rel%d" % p, m, per))
+                    trs.append(("stage", slot, via, "hand", slot, "rel%d" % p, m, per))
                     handed.setdefault(via, []).append((slot, r))
-            calls.setdefault(s, []).append(("st%d" % p, 16, trs))
+            own.setdefault(s, []).append(("st%d" % p, 16, trs))
             for h, lst in handed.items():
-                hm, hper = _deal(_pool(topo, h, [cores[r] for slot, r in lst])[::2], len(lst))
-                calls.setdefault(h, []).append(("rel%d" % p, per * len(lst),
-                                                [(slot, cores[r], "land", j, "arr%d" % j, m, hper)
-                                                 for (slot, r), m in zip(lst, hm)]))
+                hpool = _pool(topo, h, [cores[r] for slot, r in lst])
+                hm, hper = _deal(hpool if h in cores else hpool[::2], len(lst))
+                fwd.setdefault(h, []).append(("rel%d" % p, per * len(lst),
+                                              [("hand", slot, cores[r], "land", j, "arr%d" % j, m, hper)
+                                               for (slot, r), m in zip(lst, hm)]))
                 for slot, r in lst:
-                    due[r][j] = (hper, (1, p))
+                    due[r][j] = (hper, (1 if h in cores else 2, p))
+    calls = dict((c, own.get(c, []) + fwd.get(c, [])) for c in list(own) + list(fwd))
     return groups, calls, due
 
 
@@ -130,10 +137,10 @@ def rank_program(g, core, T, topo):
     for sem, count, trs in calls.get(core, []):
         g.wait_ge(S[sem], count)
         lst = []
-        for slot, dst, buf, dslot, rsem, mask, per in trs:
+        for sbuf, slot, dst, buf, dslot, rsem, mask, per in trs:
             rid, pid = topo.addr(dst, core)
             lst.append(RemoteDMATransfer(dst_ids=[DstId(rid=rid, pnc=pid)], dma_engine_mask=mask, remote_sem=S[rsem],
-                                         src=T.stage[slot], dst=T[buf][dslot]))
+                                         src=T[sbuf][slot], dst=T[buf][dslot]))
             total += per
         g.remote_dma_fused(lst, local_sem=S.sent)
 

@@ -11,13 +11,14 @@ ROWS, WID = 128, FB * TK // 128
 SCRATCH = {
     "xs": ("sbuf", [128, TK], "bfloat16"),
     "ws": ("sbuf", [128, N * FB], "bfloat16"),
-    "acc": ("psum", [128, 512 * PHASES], "float32"),
+    "acc": ("psum", [128, 512 * (PHASES + 1)], "float32"),
     "prod": ("sbuf", [128, TK * PHASES], "bfloat16"),
+    "nb": ("sbuf", [ROWS, WID], "bfloat16"),
     "stage": ("dram", [N, ROWS, WID], "bfloat16"),
     "hand": ("dram", [N - SLOTS, ROWS, WID], "bfloat16"),
     "land": ("dram", [N, ROWS, WID], "bfloat16"),
 }
-SEMAPHORES = (["ldx", "ldw", "sent", "fin0", "fin1"]
+SEMAPHORES = (["ldx", "ldw", "sent", "fin0", "fin1", "mmn", "cpn"]
               + ["%s%d" % (n, p) for n in ("mm", "cp", "st", "rel") for p in range(PHASES)]
               + ["arr%d" % j for j in range(N)])
 
@@ -63,18 +64,22 @@ def _plan(cores, topo):
         able = [h for h in world if place(h) == place(s) and h != s and all(topo.may_write(h, cores[r]) for r in barred)]
         todo = []
         for p, (a, b) in enumerate(groups[j]):
-            row = []
+            row, cold = [], 0
             for pos, r in enumerate(chips[a] + chips[b]):
-                if r == j:
+                if r in chips[me]:
                     continue
                 via = None
                 if r in barred:
                     there = [h for h in able if topo.die(h) == topo.die(cores[r])]
                     ranks = [h for h in there if h in cores]
-                    via = ranks[0] if ranks else there[p % len(there)]
+                    via = ranks[0] if ranks else there[cold % len(there)]
+                    cold += 0 if ranks else 1
                 row.append((SLOTS * p + pos, r, via))
             todo.append(row)
-        pool = _pool(topo, s, [cores[r] if via is None else via for row in todo for slot, r, via in row])
+        nb = [r for r in chips[me] if r != j][0]
+        pool = _pool(topo, s, [cores[nb]] + [cores[r] if via is None else via for row in todo for slot, r, via in row])
+        own[s] = [("cpn", 1, [("nb", None, cores[nb], "land", j, "arr%d" % j, sum(1 << e for e in pool), len(pool))])]
+        due[nb][j] = (len(pool), (-1, 0))
         for p, row in enumerate(todo):
             masks, per = _deal(pool, len(row))
             trs, handed = [], {}
@@ -85,15 +90,15 @@ def _plan(cores, topo):
                 else:
                     trs.append(("stage", slot, via, "hand", slot, "rel%d" % p, m, per))
                     handed.setdefault(via, []).append((slot, r))
-            own.setdefault(s, []).append(("st%d" % p, 16, trs))
+            own[s].append(("st%d" % p, 16, trs))
             for h, lst in handed.items():
                 hpool = _pool(topo, h, [cores[r] for slot, r in lst])
-                hm, hper = _deal(hpool if h in cores else hpool[::2], len(lst))
+                hm, hper = _deal(hpool if h in cores else hpool[::2][:2 * len(lst)], len(lst))
                 fwd.setdefault(h, []).append(("rel%d" % p, per * len(lst),
                                               [("hand", slot, cores[r], "land", j, "arr%d" % j, m, hper)
                                                for (slot, r), m in zip(lst, hm)]))
                 for slot, r in lst:
-                    due[r][j] = (hper, (1 if h in cores else 2, p))
+                    due[r][j] = (hper, (1, p))
     calls = dict((c, own.get(c, []) + fwd.get(c, [])) for c in list(own) + list(fwd))
     return groups, calls, due
 
@@ -125,6 +130,14 @@ def rank_program(g, core, T, topo):
             q = queues[p % 2]
             q.wait_ge(S["cp%d" % p], 1)
             q.dma_start(out=T.stage[SLOTS * p:SLOTS * (p + 1)], in_=prod).then_inc(S["st%d" % p], 16)
+            if p == 0:
+                nb = [r for r in range(N) if r // PER_CHIP == rank // PER_CHIP and r != rank][0]
+                n0 = 512 * PHASES
+                for qd in range(TK // WID):
+                    g.tensor.matmul(T.acc[FB * qd:FB * (qd + 1), n0:n0 + WID], T.ws[:, FB * nb:FB * (nb + 1)],
+                                    T.xs[:, WID * qd:WID * (qd + 1)], start=True, stop=True).then_inc(S.mmn, 1)
+                g.vector.wait_ge(S.mmn, TK // WID)
+                g.vector.tensor_copy(out=T.nb[:], in_=T.acc[:, n0:n0 + WID]).then_inc(S.cpn, 1)
         p = PHASES - 1
         pos = PER_CHIP * groups[rank][p].index(rank // PER_CHIP) + rank % PER_CHIP
         qi = (p + 1) % 2
@@ -140,13 +153,22 @@ def rank_program(g, core, T, topo):
         for sbuf, slot, dst, buf, dslot, rsem, mask, per in trs:
             rid, pid = topo.addr(dst, core)
             lst.append(RemoteDMATransfer(dst_ids=[DstId(rid=rid, pnc=pid)], dma_engine_mask=mask, remote_sem=S[rsem],
-                                         src=T[sbuf][slot], dst=T[buf][dslot]))
+                                         src=T[sbuf][:] if slot is None else T[sbuf][slot], dst=T[buf][dslot]))
             total += per
         g.remote_dma_fused(lst, local_sem=S.sent)
 
     if rank is not None:
         order = sorted(due[rank], key=lambda j: (due[rank][j][1], j))
         for i, j in enumerate(order):
+            if due[rank][j][1][0] < 0:
+                for q in queues:
+                    q.wait_ge(S["arr%d" % j], due[rank][j][0])
+                for qd in range(TK // WID):
+                    c0 = TK * j + WID * qd
+                    queues[qd % 2].dma_start(out=T.y[:, c0:c0 + WID],
+                                             in_=T.land[j, FB * qd:FB * (qd + 1), :]).then_inc(S["fin%d" % (qd % 2)], 16)
+                    stores[qd % 2] += 1
+                continue
             qi = i % 2
             queues[qi].wait_ge(S["arr%d" % j], due[rank][j][0])
             queues[qi].dma_start(out=T.y[:, TK * j:TK * (j + 1)], in_=T.land[j]).then_inc(S["fin%d" % qi], 16)

from concourse.bass import DstId, RemoteDMATransfer

N, FB, TK = 12, 32, 256
PER_CHIP = 2
NCHIP = N // PER_CHIP
PHASES = NCHIP // 2
SLOTS = 2 * PER_CHIP
CW = PER_CHIP * FB
ROWS, WID = 128, FB * TK // 128

SCRATCH = {
    "xs": ("sbuf", [128, TK], "bfloat16"),
    "ws": ("sbuf", [128, N * FB], "bfloat16"),
    "acc": ("psum", [128, 512 * (PHASES + 1)], "float32"),
    "prod": ("sbuf", [128, TK * PHASES], "bfloat16"),
    "nb": ("sbuf", [ROWS, WID], "bfloat16"),
    "stage": ("dram", [N, ROWS, WID], "bfloat16"),
    "hand": ("dram", [N - SLOTS, ROWS, WID], "bfloat16"),
    "land": ("dram", [N, ROWS, WID], "bfloat16"),
}
SEMAPHORES = (["ldx", "ldw", "sent", "fin0", "fin1", "mmn", "cpn"]
              + ["%s%d" % (n, p) for n in ("mm", "cp", "st", "rel") for p in range(PHASES)]
              + ["arr%d" % j for j in range(N)])


def _pool(topo, src, dsts):
    mask = topo.mask(src, dsts[0])
    for d in dsts:
        mask &= topo.mask(src, d)
    return [e for e in range(mask.bit_length()) if (mask >> e) & 1]


def _deal(pool, k):
    per = 1
    while per * 2 * k <= len(pool):
        per *= 2
    return [sum(1 << e for e in pool[i * per:(i + 1) * per]) for i in range(k)], per


def _plan(cores, topo):
    def place(c):
        return (topo.host(c), topo.chip(c))
    chips = [list(range(i, i + PER_CHIP)) for i in range(0, N, PER_CHIP)]
    rep = [cores[m[0]] for m in chips]
    world = range((max(topo.host(c) for c in cores) + 1) * topo.CORES_PER_HOST)
    groups, own, fwd, due = {}, {}, {}, dict((r, {}) for r in range(N))
    for j, s in enumerate(cores):
        me = j // PER_CHIP
        plane = [i for i in range(NCHIP) if i == me or topo.same_plane(rep[i], rep[me])]
        far = [i for i in range(NCHIP) if i not in plane]
        k = plane.index(me)
        near = [plane[(k + t) % len(plane)] for t in range(1, len(plane))]
        off = k * len(far) // len(plane)
        far = [far[(off + t) % len(far)] for t in range(len(far))]
        barred = [r for r in range(N) if r != j and not topo.may_write(s, cores[r])]
        if barred:
            seq = far + near
        else:
            at = [t * (NCHIP - 2) // len(far) for t in range(len(far))]
            rest = list(near)
            seq = [far[at.index(t)] if t in at else rest.pop(0) for t in range(NCHIP - 1)]
        seq = seq + [me]
        groups[j] = [tuple(sorted(seq[2 * p:2 * p + 2])) for p in range(PHASES)]
        able = [h for h in world if place(h) == place(s) and h != s and all(topo.may_write(h, cores[r]) for r in barred)]
        todo = []
        for p, (a, b) in enumerate(groups[j]):
            row, cold = [], 0
            for pos, r in enumerate(chips[a] + chips[b]):
                if r in chips[me]:
                    continue
                via = None
                if r in barred:
                    there = [h for h in able if topo.die(h) == topo.die(cores[r])]
                    ranks = [h for h in there if h in cores]
                    via = ranks[0] if ranks else there[cold % len(there)]
                    cold += 0 if ranks else 1
                row.append((SLOTS * p + pos, r, via))
            todo.append(row)
        nb = [r for r in chips[me] if r != j][0]
        pool = _pool(topo, s, [cores[nb]] + [cores[r] if via is None else via for row in todo for slot, r, via in row])
        own[s] = [("cpn", 1, [("nb", None, cores[nb], "land", j, "arr%d" % j, sum(1 << e for e in pool), len(pool))])]
        due[nb][j] = (len(pool), (-1, 0))
        for p, row in enumerate(todo):
            masks, per = _deal(pool, len(row))
            trs, handed = [], {}
            for (slot, r, via), m in zip(row, masks):
                if via is None:
                    trs.append(("stage", slot, cores[r], "land", j, "arr%d" % j, m, per))
                    due[r][j] = (per, (0, p))
                else:
                    trs.append(("stage", slot, via, "hand", slot, "rel%d" % p, m, per))
                    handed.setdefault(via, []).append((slot, r))
            own[s].append(("st%d" % p, 16, trs))
            for h, lst in handed.items():
                hpool = _pool(topo, h, [cores[r] for slot, r in lst])
                hm, hper = _deal(hpool if h in cores else hpool[::2][:2 * len(lst)], len(lst))
                fwd.setdefault(h, []).append(("rel%d" % p, per * len(lst),
                                              [("hand", slot, cores[r], "land", j, "arr%d" % j, m, hper)
                                               for (slot, r), m in zip(lst, hm)]))
                for slot, r in lst:
                    due[r][j] = (hper, (1, p))
    calls = dict((c, own.get(c, []) + fwd.get(c, [])) for c in list(own) + list(fwd))
    return groups, calls, due


def rank_program(g, core, T, topo):
    groups, calls, due = _plan(T.cores, topo)
    S = T.sem
    rank = T.rank_of(core)
    queues = (g.sync, g.scalar)
    stores = [0, 0]

    if rank is not None:
        g.sync.dma_start(out=T.xs[:], in_=T.x[:]).then_inc(S.ldx, 16)
        g.scalar.dma_start(out=T.ws[:], in_=T.w[:]).then_inc(S.ldw, 16)
        g.tensor.wait_ge(S.ldx, 16)
        g.tensor.wait_ge(S.ldw, 16)
        for p, (a, b) in enumerate(groups[rank]):
            c0, c1 = 512 * p, 512 * p + TK
            prod = T.prod[:, TK * p:TK * (p + 1)]
            if b == a + 1:
                parts = [(0, 2 * CW, a)]
            else:
                parts = [(0, CW, a), (CW, CW, b)]
            for row, m, chip in parts:
                g.tensor.matmul(T.acc[row:row + m, c0:c1], T.ws[:, CW * chip:CW * chip + m], T.xs[:],
                                start=True, stop=True).then_inc(S["mm%d" % p], 1)
            g.vector.wait_ge(S["mm%d" % p], len(parts))
            g.vector.tensor_copy(out=prod, in_=T.acc[:, c0:c1]).then_inc(S["cp%d" % p], 1)
            q = queues[p % 2]
            q.wait_ge(S["cp%d" % p], 1)
            q.dma_start(out=T.stage[SLOTS * p:SLOTS * (p + 1)], in_=prod).then_inc(S["st%d" % p], 16)
            if p == 0:
                nb = [r for r in range(N) if r // PER_CHIP == rank // PER_CHIP and r != rank][0]
                n0 = 512 * PHASES
                for qd in range(TK // WID):
                    g.tensor.matmul(T.acc[FB * qd:FB * (qd + 1), n0:n0 + WID], T.ws[:, FB * nb:FB * (nb + 1)],
                                    T.xs[:, WID * qd:WID * (qd + 1)], start=True, stop=True).then_inc(S.mmn, 1)
                g.vector.wait_ge(S.mmn, TK // WID)
                g.vector.tensor_copy(out=T.nb[:], in_=T.acc[:, n0:n0 + WID]).then_inc(S.cpn, 1)
        p = PHASES - 1
        pos = PER_CHIP * groups[rank][p].index(rank // PER_CHIP) + rank % PER_CHIP
        qi = (p + 1) % 2
        queues[qi].wait_ge(S["cp%d" % p], 1)
        queues[qi].dma_start(out=T.y[:, TK * rank:TK * (rank + 1)],
                             in_=T.prod[FB * pos:FB * (pos + 1), TK * p:TK * (p + 1)]).then_inc(S["fin%d" % qi], 16)
        stores[qi] += 1

    total = 0
    for sem, count, trs in calls.get(core, []):
        g.wait_ge(S[sem], count)
        lst = []
        for sbuf, slot, dst, buf, dslot, rsem, mask, per in trs:
            rid, pid = topo.addr(dst, core)
            lst.append(RemoteDMATransfer(dst_ids=[DstId(rid=rid, pnc=pid)], dma_engine_mask=mask, remote_sem=S[rsem],
                                         src=T[sbuf][:] if slot is None else T[sbuf][slot], dst=T[buf][dslot]))
            total += per
        g.remote_dma_fused(lst, local_sem=S.sent)

    if rank is not None:
        order = sorted(due[rank], key=lambda j: (due[rank][j][1], j))
        for i, j in enumerate(order):
            if due[rank][j][1][0] < 0:
                for q in queues:
                    q.wait_ge(S["arr%d" % j], due[rank][j][0])
                for qd in range(TK // WID):
                    c0 = TK * j + WID * qd
                    queues[qd % 2].dma_start(out=T.y[:, c0:c0 + WID],
                                             in_=T.land[j, FB * qd:FB * (qd + 1), :]).then_inc(S["fin%d" % (qd % 2)], 16)
                    stores[qd % 2] += 1
                continue
            qi = i % 2
            queues[qi].wait_ge(S["arr%d" % j], due[rank][j][0])
            queues[qi].dma_start(out=T.y[:, TK * j:TK * (j + 1)], in_=T.land[j]).then_inc(S["fin%d" % qi], 16)
            stores[qi] += 1
        for qi in (0, 1):
            queues[qi].wait_ge(S["fin%d" % qi], 16 * stores[qi])
    if total:
        g.wait_ge(S.sent, total)
